import numpy as np
import ml_dtypes


def mxq(x, axis, fmt="e4m3"):
    dtype, down = {"e4m3": (ml_dtypes.float8_e4m3fn, 7), "e5m2": (ml_dtypes.float8_e5m2, 14)}[fmt]
    v = np.moveaxis(np.asarray(x, np.float32).astype(ml_dtypes.bfloat16).astype(np.float64), axis, -1)
    blocks = v.reshape(v.shape[:-1] + (-1, 32))
    amax = np.abs(blocks).max(-1, keepdims=True)
    byte = np.maximum(np.where(amax > 0, np.frexp(amax)[1] - 1 + 127, 0) - down, 1)
    scale = np.exp2(byte - 127.0)
    codes = (blocks / scale).astype(np.float32).astype(dtype).astype(np.float64)
    return np.moveaxis((codes * scale).reshape(v.shape), -1, axis)


WIDE = False


def mx_kscale(k):
    if not WIDE:
        return np.ones(k)
    levels = np.array([10, -10, 5, -5, 0])
    if k % 512:
        return np.exp2(np.random.permutation(np.resize(levels, k // 32))).repeat(32)
    a = np.empty((k // 512, 16))
    for p in range(k // 512):
        a[p, :8] = np.random.permutation(np.resize(levels, 8))
        for g in range(8):
            far = levels[np.abs(levels - a[p, g]) >= 10]
            a[p, g + 8] = far[np.random.randint(len(far))]
    return np.exp2(a.ravel()).repeat(32)


def f64(x):
    return np.asarray(x).astype(np.float64)


def striped(idx):
    return np.tile(idx.reshape(-1, 16).T, (8, 1)).astype(np.uint16)


def unstriped(offs):
    return offs[:16].T.reshape(-1).astype(np.int64)


def striped8(idx):
    return np.concatenate([x.reshape(-1, 16).T for x in idx]).astype(np.uint16)


def runs(offs, k):
    lists = np.stack([offs[16 * r : 16 * r + 16].T.reshape(-1) for r in range(8)]).astype(np.int64)
    return lists[np.arange(k) % 512 // 64]


def pack_weight(w):
    k, n = w.shape
    w = f64(np.asarray(w, np.float32).astype(ml_dtypes.bfloat16)).reshape(k // 32, 32, n)
    amax = np.abs(w).max(1)
    byte = np.clip(np.where(amax > 0, np.frexp(amax)[1] - 1 + 127 - 7, 1), 1, 254)
    scaled = (w * np.exp2(127.0 - byte)[:, None, :]).reshape(k, n).astype(np.float32)
    words = np.ascontiguousarray(scaled.reshape(k // 512, 128, 4, n).transpose(0, 1, 3, 2)).astype(ml_dtypes.float8_e4m3fn).view(np.uint8)
    return words, np.ascontiguousarray(byte.astype(np.uint8).reshape(k // 512, 16, n))


def unpack_weight(words, scales):
    g, p, n, _ = words.shape
    vals = np.ascontiguousarray(words).view(ml_dtypes.float8_e4m3fn).astype(np.float64) * np.repeat(np.exp2(scales.astype(np.float64) - 127.0), 8, axis=1)[..., None]
    return vals.transpose(0, 1, 3, 2).reshape(g * 512, n)


def sigmoid(v):
    return 1.0 / (1.0 + np.exp(-np.maximum(v, -700.0)))

def planes(y):
    n, m = y.shape
    v = y.astype(np.float32).astype(ml_dtypes.bfloat16).astype(np.float64).reshape(n // 32, 32, m)
    top = np.abs(v).max(1)
    byte = np.clip(np.where(top > 0, np.frexp(top)[1] - 1 + 127 - 7, 1), 1, 254)
    codes = (v * np.exp2(127.0 - byte)[:, None, :]).reshape(n, m).astype(np.float32).astype(ml_dtypes.float8_e4m3fn).view(np.uint8)
    words = codes.reshape(n // 512, 128, 4, m).transpose(0, 1, 3, 2)
    return np.ascontiguousarray(words), np.ascontiguousarray(byte.astype(np.uint8).reshape(n // 512, 16, m))


K, T, S, N, H = 512, 2048, 512, 512, 512


def setup_inputs():
    n = np.random.standard_normal
    s = mx_kscale(K)[:, None]
    u = mx_kscale(H)
    packed_xT = pack_weight(n((K, T)) * s)
    packed_w1 = pack_weight(n((K, H)) / np.sqrt(K) / s)
    packed_w2 = pack_weight(n((H, N)) / np.sqrt(H) / u[:, None])
    packed_w3 = pack_weight(n((H, N)) / np.sqrt(H) / u[:, None])
    return {
        "x_words": packed_xT[0],
        "x_scales": packed_xT[1],
        "w1_words": packed_w1[0],
        "w1_scales": packed_w1[1],
        "gn": (np.random.uniform(0.5, 1.5, (H, 1)) * u[:, None]).astype(np.float32),
        "w2_words": packed_w2[0],
        "w2_scales": packed_w2[1],
        "gm": (np.random.uniform(0.5, 1.5, (H, 1)) * u[:, None]).astype(np.float32),
        "w3_words": packed_w3[0],
        "w3_scales": packed_w3[1],
        "offs": striped(np.random.permutation(T)[:S]),
        "n1": striped8(np.stack([np.random.permutation(S) for _ in range(8)])),
        "n2": striped8(np.stack([np.random.permutation(S) for _ in range(8)])),
        "n3": striped8(np.stack([np.random.permutation(S) for _ in range(8)])),
        "n4": striped8(np.stack([np.random.permutation(S) for _ in range(8)])),
        "n5": striped8(np.stack([np.random.permutation(S) for _ in range(8)])),
        "n6": striped8(np.stack([np.random.permutation(S) for _ in range(8)])),
    }


def reference(x_words, x_scales, w1_words, w1_scales, gn, w2_words, w2_scales, gm, w3_words, w3_scales, offs, n1, n2, n3, n4, n5, n6):
    xq = unpack_weight(x_words, x_scales)[:, unstriped(offs)]
    y = unpack_weight(w1_words, w1_scales).T @ xq
    st = y + 0.5 * (y[np.arange(H)[:, None], runs(n1, H)])
    z = f64(gn) * (st - (st[np.arange(H)[:, None], runs(n2, H)]))
    a = unpack_weight(w2_words, w2_scales).T @ mxq(z, 0, "e4m3")
    pa = y[np.arange(H)[:, None], runs(n3, H)]
    pb = y[np.arange(H)[:, None], runs(n4, H)]
    z2 = f64(gm) * (np.maximum(np.minimum(y, pa), np.minimum(np.maximum(y, pa), pb)))
    b = unpack_weight(w3_words, w3_scales).T @ mxq(z2, 0, "e4m3")
    out_0 = a + (sigmoid(b[np.arange(N)[:, None], runs(n6, N)] - b)) * (a[np.arange(N)[:, None], runs(n5, N)] - a)
    return (out_0,) + planes(out_0)

@@ -1,0 +1,233 @@
+from contextlib import ExitStack
+
+import concourse.mybir as mybir
+
+K, T, S, N, H = 512, 2048, 512, 512, 512
+FLOPS = 2 * K * H * S + 2 * 2 * H * N * S
+
+F32 = mybir.dt.float32
+BF16 = mybir.dt.bfloat16
+I32 = mybir.dt.int32
+U32 = mybir.dt.uint32
+U16 = mybir.dt.uint16
+U8 = mybir.dt.uint8
+FP8X4 = mybir.dt.float8_e4m3fn_x4
+ALU = mybir.AluOpType
+ACT = mybir.ActivationFunctionType
+
+P = 128
+PACK = 4
+WIDE = 2 * S
+CHUNKS = ((0, 128), (128, 256), (256, 384), (384, 512))
+
+
+def words_of(packed):
+    return packed[0].rearrange("p n t -> p (n t)").bitcast(I32)
+
+
+def tile_picked_forkpullbhopmed_none_po_kernel(
+    tc, x_words, x_scales, w1_words, w1_scales, gn, w2_words, w2_scales, gm, w3_words, w3_scales,
+    offs, n1, n2, n3, n4, n5, n6, out_0, out_1, out_2,
+):
+    nc = tc.nc
+    with ExitStack() as ctx:
+        keep = ctx.enter_context(tc.tile_pool(name="keep", bufs=1))
+        ring = ctx.enter_context(tc.tile_pool(name="ring", bufs=2))
+        psum = ctx.enter_context(tc.psum_pool(name="psum", bufs=1))
+
+        def sb(name, shape, dtype, tag=None):
+            return keep.tile(shape, dtype, name=name, tag=tag or name, align_bytes=64)
+
+        def planes(name, width, dtype=F32):
+            return [sb("%s%d" % (name, t), [P, width], dtype) for t in range(PACK)]
+
+        lists = {name: keep.tile([P, S // 16], U16, name="list_" + name)
+                 for name in ("offs", "n1", "n2", "n3", "n4", "n5", "n6")}
+
+        def load_scale_rows(queue, plane, scales, first):
+            for q in range(4):
+                queue.dma_start(plane[32 * q + first : 32 * q + first + 4, :].bitcast(I32),
+                                scales[0, 4 * q : 4 * q + 4, :].bitcast(I32))
+
+        def deal_words(dealt, raw):
+            nc.vector.tensor_copy(
+                dealt[:].bitcast(U32).rearrange("p (t b i) -> p b t i", t=PACK, i=4),
+                raw[:].bitcast(U32).rearrange("p (b i t) -> p b t i", t=PACK, i=4))
+
+        def deal_scales(dealt, raw):
+            nc.vector.tensor_copy(
+                dealt[:].rearrange("p (t b i) -> p b t i", t=PACK, i=16),
+                raw[:].rearrange("p (b i t) -> p b t i", t=PACK, i=16))
+
+        def interleave(engine_copy, grouped, by_plane):
+            engine_copy(grouped[:].rearrange("p (c i t) -> p c t i", t=PACK, i=4),
+                        by_plane.rearrange("p t (c i) -> p c t i", i=4))
+
+        def product(bank, t, w_dealt, w_plane, first, codes, scales):
+            cols = slice(t * P, (t + 1) * P)
+            nc.tensor.matmul_mx(bank[:], lhsT=w_dealt[:, cols].bitcast(FP8X4), lhsT_scale=w_plane[first:, cols],
+                                rhs=codes[:].bitcast(FP8X4), rhs_scale=scales[:], start=True, stop=True)
+
+        x_raw = sb("x_raw", [P, T], I32)
+        xs_raw = sb("xs_raw", [P, T], U8)
+        w1_raw = sb("w1_raw", [P, H], I32)
+        w2_raw = sb("w2_raw", [P, N], I32)
+        w3_raw = sb("w3_raw", [P, N], I32)
+        w1s_raw = sb("w1s_raw", [P, H], U8)
+        w23s_raw = sb("w23s_raw", [P, N], U8)
+        gn_sb = sb("gn_sb", [P, PACK], F32)
+        gm_sb = sb("gm_sb", [P, PACK], F32)
+        warm = sb("warm", [P, 1], F32)
+
+        nc.vector.memset(xs_raw[:].bitcast(I32), 0)
+        nc.vector.memset(w1s_raw[:].bitcast(I32), 0)
+        nc.vector.memset(w23s_raw[:].bitcast(I32), 0)
+        nc.vector.memset(warm[:], 0.0)
+        nc.scalar.activation(warm[:], warm[:], ACT.Sigmoid)
+
+        nc.sync.dma_start(lists["offs"][:], offs)
+        nc.sync.dma_start(x_raw[:, : T // 2], words_of(x_words)[:, : T // 2])
+        load_scale_rows(nc.sync, xs_raw, x_scales, 0)
+        nc.sync.dma_start(x_raw[:, T // 2 :], words_of(x_words)[:, T // 2 :])
+        nc.sync.dma_start(w1_raw[:], words_of(w1_words))
+        load_scale_rows(nc.sync, w1s_raw, w1_scales, 0)
+        nc.sync.dma_start(gm_sb[:], gm.rearrange("(p t) o -> p (t o)", t=PACK))
+        nc.sync.dma_start(lists["n3"][:], n3)
+        nc.sync.dma_start(w3_raw[:], words_of(w3_words))
+        nc.sync.dma_start(w2_raw[:], words_of(w2_words))
+        nc.sync.dma_start(lists["n4"][:], n4)
+        nc.sync.dma_start(gn_sb[:], gn.rearrange("(p t) o -> p (t o)", t=PACK))
+        load_scale_rows(nc.sync, w23s_raw, w3_scales, 8)
+        load_scale_rows(nc.sync, w23s_raw, w2_scales, 4)
+        nc.sync.dma_start(lists["n1"][:], n1)
+        nc.sync.dma_start(lists["n2"][:], n2)
+        nc.sync.dma_start(lists["n6"][:], n6)
+        nc.sync.dma_start(lists["n5"][:], n5)
+
+        w1_dealt = sb("w1_dealt", [P, H], I32)
+        w2_dealt = sb("w2_dealt", [P, N], I32)
+        w3_dealt = sb("w3_dealt", [P, N], I32)
+        w1s = sb("w1s", [P, H], U8)
+        w23s = sb("w23s", [P, N], U8)
+        x_codes = sb("x_codes", [P, S], I32)
+        x_plane = sb("x_plane", [P, S], U8)
+
+        nc.vector.tensor_copy(x_plane[:], xs_raw[:].indirect(lists["offs"][:]))
+        nc.vector.tensor_copy(x_codes[:].bitcast(U32), x_raw[:].bitcast(U32).indirect(lists["offs"][:]))
+        deal_words(w1_dealt, w1_raw)
+        deal_scales(w1s, w1s_raw)
+
+        banks = [psum.tile([P, S], F32, name="bank%d" % b) for b in range(2 * PACK)]
+        y_ps, b_ps = banks[:PACK], banks[PACK:]
+        for t in range(PACK):
+            product(y_ps[t], t, w1_dealt, w1s, 0, x_codes, x_plane)
+
+        gains = sb("gains", [P, 2, PACK], F32)
+        nc.vector.tensor_scalar(gains[:, 0, :], gn_sb[:], -0.5, None, ALU.mult)
+        nc.vector.tensor_scalar(gains[:, 1, :], gn_sb[:], -1.0, None, ALU.mult)
+        deal_words(w3_dealt, w3_raw)
+        deal_words(w2_dealt, w2_raw)
+        deal_scales(w23s, w23s_raw)
+
+        ym = planes("ym", WIDE)
+        ym16 = sb("ym16", [P, PACK, S], BF16)
+        pa = sb("pa", [P, PACK, S], BF16)
+        pb = sb("pb", [P, PACK, S], BF16)
+        for t in range(PACK):
+            nc.scalar.activation(ym[t][:, :S], y_ps[t][:], ACT.Copy, scale=gm_sb[:, t : t + 1])
+        yh = planes("yh", WIDE)
+        yn = planes("yn", S)
+        for t in range(PACK):
+            nc.scalar.activation(ym16[:, t, :], y_ps[t][:], ACT.Copy, scale=gm_sb[:, t : t + 1])
+        for t in range(PACK):
+            nc.scalar.activation(yh[t][:, :S], y_ps[t][:], ACT.Copy, scale=gains[:, 0, t : t + 1])
+            nc.scalar.activation(yn[t][:], y_ps[t][:], ACT.Copy, scale=gains[:, 1, t : t + 1])
+        for t in range(PACK):
+            nc.vector.tensor_copy(pa[:, t, :], ym[t][:].indirect(lists["n3"][:]))
+            nc.vector.tensor_copy(pb[:, t, :], ym[t][:].indirect(lists["n4"][:]))
+
+        st = planes("st", WIDE)
+        st_again = planes("st_again", S)
+
+        def pull(t):
+            nc.vector.tensor_tensor(st[t][:, :S], yh[t][:].indirect(lists["n1"][:]), yn[t][:], ALU.add)
+            nc.sync.dma_start(st_again[t][:], st[t][:, :S])
+
+        lo = sb("lo", [P, PACK, S], BF16)
+        hi = sb("hi", [P, PACK, S], BF16)
+        mid = sb("mid", [P, PACK, S], BF16)
+        z2 = sb("z2", [P, PACK, S], BF16)
+        nc.vector.tensor_tensor(hi[:], pa[:], pb[:], ALU.max)
+        nc.vector.tensor_tensor(lo[:], pa[:], pb[:], ALU.min)
+        nc.vector.tensor_tensor(mid[:], hi[:], ym16[:], ALU.min)
+        pull(0)
+        nc.vector.tensor_tensor(z2[:], lo[:], mid[:], ALU.max)
+        z2_grouped = sb("z2_grouped", [P, PACK * S], BF16)
+        interleave(nc.scalar.copy, z2_grouped, z2[:])
+        for t in range(1, PACK):
+            pull(t)
+
+
+        def hop(t):
+            nc.vector.tensor_tensor(z[:, t, :], st[t][:].indirect(lists["n2"][:]), st_again[t][:], ALU.subtract)
+
+        z2_codes = sb("z2_codes", [P, S], I32)
+        z2_plane = sb("z2_plane", [P, S], U8)
+        nc.vector.quantize_mx(z2_codes[:].bitcast(FP8X4), z2_plane[:], z2_grouped[:])
+        z = sb("z", [P, PACK, S], F32, tag="z2_grouped")
+        bw = planes("bw", WIDE)
+        b_again = planes("b_again", S)
+        for t in range(PACK):
+            product(b_ps[t], t, w3_dealt, w23s, 8, z2_codes, z2_plane)
+        for t in range(PACK):
+            nc.scalar.copy(bw[t][:, :S], b_ps[t][:])
+            nc.sync.dma_start(b_again[t][:], bw[t][:, :S])
+        for t in range(PACK):
+            hop(t)
+        z_grouped = sb("z_grouped", [P, PACK * S], BF16)
+        interleave(nc.scalar.copy, z_grouped, z[:])
+
+        u = [sb("u%d" % t, [P, S], F32) for t in range(PACK - 1)]
+        gate = planes("gate", S)
+
+        def gating(t):
+            nc.vector.tensor_tensor(u[t][:], bw[t][:].indirect(lists["n6"][:]), b_again[t][:], ALU.subtract)
+            nc.scalar.activation(gate[t][:], u[t][:], ACT.Sigmoid)
+
+        for t in range(PACK - 1):
+            gating(t)
+        z_codes = sb("z_codes", [P, S], I32)
+        z_plane = sb("z_plane", [P, S], U8)
+        nc.vector.quantize_mx(z_codes[:].bitcast(FP8X4), z_plane[:], z_grouped[:])
+        u.append(sb("u_last", [P, S], F32, tag="z_grouped"))
+        gating(PACK - 1)
+        a_ps = y_ps
+        for t in range(PACK):
+            product(a_ps[t], t, w2_dealt, w23s, 4, z_codes, z_plane)
+        aw = planes("aw", S)
+        own = sb("own", [P, PACK, S], F32)
+        for t in range(PACK):
+            nc.scalar.copy(aw[t][:], a_ps[t][:])
+
+        out_rows = out_0.rearrange("(p t) j -> p t j", t=PACK)
+        out_words = words_of(out_1)
+        out_plane = sb("out_plane", [P, S], U8)
+        for c, (j0, j1) in enumerate(CHUNKS):
+            width = j1 - j0
+            other = ring.tile([P, PACK, width], F32, name="other")
+            res = sb("res%d" % c, [P, PACK, width], F32)
+            res_grouped = sb("res_grouped%d" % c, [P, PACK * width], BF16)
+            res_codes = sb("res_codes%d" % c, [P, width], I32)
+            for t in range(PACK):
+                nc.vector.tensor_tensor(other[:, t, :], aw[t][:].indirect(lists["n5"][:, j0 // 16 : j1 // 16]),
+                                        gate[t][:, j0:j1], ALU.mult)
+                if c == 0:
+                    nc.vector.scalar_tensor_tensor(own[:, t, :], gate[t][:], 1.0, aw[t][:], ALU.subtract, ALU.mult)
+            nc.vector.tensor_tensor(res[:], other[:], own[:, :, j0:j1], ALU.subtract)
+            nc.sync.dma_start(out_rows[:, :, j0:j1], res[:])
+            interleave(nc.scalar.copy, res_grouped, res[:])
+            nc.vector.quantize_mx(res_codes[:].bitcast(FP8X4), out_plane[:, j0:j1], res_grouped[:])
+            nc.sync.dma_start(out_words[:, j0:j1], res_codes[:])
+        for q in range(4):
+            nc.sync.dma_start(out_2[0, 4 * q : 4 * q + 4, :].bitcast(I32),
+                              out_plane[32 * q : 32 * q + 4, :].bitcast(I32))

@@ -19,6 +19,11 @@ P = 128
 PACK = 4
 WIDE = 2 * S
 CHUNKS = ((0, 128), (128, 256), (256, 384), (384, 512))
+HALVES = (slice(0, S // 2), slice(S // 2, S))
+
+
+def entries(cols):
+    return slice(cols.start // 16, cols.stop // 16)
 
 
 def words_of(packed):
@@ -60,13 +65,13 @@ def tile_picked_forkpullbhopmed_none_po_kernel(
                 raw[:].rearrange("p (b i t) -> p b t i", t=PACK, i=16))
 
         def interleave(engine_copy, grouped, by_plane):
-            engine_copy(grouped[:].rearrange("p (c i t) -> p c t i", t=PACK, i=4),
+            engine_copy(grouped.rearrange("p (c i t) -> p c t i", t=PACK, i=4),
                         by_plane.rearrange("p t (c i) -> p c t i", i=4))
 
-        def product(bank, t, w_dealt, w_plane, first, codes, scales):
+        def product(result, t, w_dealt, w_plane, first, codes, scales):
             cols = slice(t * P, (t + 1) * P)
-            nc.tensor.matmul_mx(bank[:], lhsT=w_dealt[:, cols].bitcast(FP8X4), lhsT_scale=w_plane[first:, cols],
-                                rhs=codes[:].bitcast(FP8X4), rhs_scale=scales[:], start=True, stop=True)
+            nc.tensor.matmul_mx(result, lhsT=w_dealt[:, cols].bitcast(FP8X4), lhsT_scale=w_plane[first:, cols],
+                                rhs=codes.bitcast(FP8X4), rhs_scale=scales, start=True, stop=True)
 
         x_raw = sb("x_raw", [P, T], I32)
         xs_raw = sb("xs_raw", [P, T], U8)
@@ -91,9 +96,9 @@ def tile_picked_forkpullbhopmed_none_po_kernel(
         nc.sync.dma_start(x_raw[:, T // 2 :], words_of(x_words)[:, T // 2 :])
         nc.sync.dma_start(w1_raw[:], words_of(w1_words))
         load_scale_rows(nc.sync, w1s_raw, w1_scales, 0)
+        nc.sync.dma_start(w3_raw[:], words_of(w3_words))
         nc.sync.dma_start(gm_sb[:], gm.rearrange("(p t) o -> p (t o)", t=PACK))
         nc.sync.dma_start(lists["n3"][:], n3)
-        nc.sync.dma_start(w3_raw[:], words_of(w3_words))
         nc.sync.dma_start(w2_raw[:], words_of(w2_words))
         nc.sync.dma_start(lists["n4"][:], n4)
         nc.sync.dma_start(gn_sb[:], gn.rearrange("(p t) o -> p (t o)", t=PACK))
@@ -113,97 +118,116 @@ def tile_picked_forkpullbhopmed_none_po_kernel(
         x_plane = sb("x_plane", [P, S], U8)
 
         nc.vector.tensor_copy(x_plane[:], xs_raw[:].indirect(lists["offs"][:]))
-        nc.vector.tensor_copy(x_codes[:].bitcast(U32), x_raw[:].bitcast(U32).indirect(lists["offs"][:]))
+
+        def pick_words(cols):
+            nc.vector.tensor_copy(x_codes[:, cols].bitcast(U32),
+                                  x_raw[:].bitcast(U32).indirect(lists["offs"][:, entries(cols)]))
+
+        pick_words(HALVES[0])
         deal_words(w1_dealt, w1_raw)
         deal_scales(w1s, w1s_raw)
+        pick_words(HALVES[1])
 
         banks = [psum.tile([P, S], F32, name="bank%d" % b) for b in range(2 * PACK)]
         y_ps, b_ps = banks[:PACK], banks[PACK:]
+        y_parts = [[(cols, bank[:, cols]) for cols, bank in zip(HALVES, (y_ps[0], b_ps[0]))]]
+        y_parts.extend([(slice(0, S), y_ps[t][:])] for t in range(1, PACK))
         for t in range(PACK):
-            product(y_ps[t], t, w1_dealt, w1s, 0, x_codes, x_plane)
+            for cols, result in y_parts[t]:
+                product(result, t, w1_dealt, w1s, 0, x_codes[:, cols], x_plane[:, cols])
+
+        def scaled_y(row, t, gain):
+            for cols, result in y_parts[t]:
+                nc.scalar.activation(row[:, cols], result, ACT.Copy, scale=gain)
 
         gains = sb("gains", [P, 2, PACK], F32)
         nc.vector.tensor_scalar(gains[:, 0, :], gn_sb[:], -0.5, None, ALU.mult)
         nc.vector.tensor_scalar(gains[:, 1, :], gn_sb[:], -1.0, None, ALU.mult)
         deal_words(w3_dealt, w3_raw)
         deal_words(w2_dealt, w2_raw)
-        deal_scales(w23s, w23s_raw)
 
         ym = planes("ym", WIDE)
         ym16 = sb("ym16", [P, PACK, S], BF16)
         pa = sb("pa", [P, PACK, S], BF16)
         pb = sb("pb", [P, PACK, S], BF16)
         for t in range(PACK):
-            nc.scalar.activation(ym[t][:, :S], y_ps[t][:], ACT.Copy, scale=gm_sb[:, t : t + 1])
+            scaled_y(ym[t], t, gm_sb[:, t : t + 1])
         yh = planes("yh", WIDE)
         yn = planes("yn", S)
         for t in range(PACK):
-            nc.scalar.activation(ym16[:, t, :], y_ps[t][:], ACT.Copy, scale=gm_sb[:, t : t + 1])
+            scaled_y(ym16[:, t, :], t, gm_sb[:, t : t + 1])
         for t in range(PACK):
-            nc.scalar.activation(yh[t][:, :S], y_ps[t][:], ACT.Copy, scale=gains[:, 0, t : t + 1])
-            nc.scalar.activation(yn[t][:], y_ps[t][:], ACT.Copy, scale=gains[:, 1, t : t + 1])
-        for t in range(PACK):
-            nc.vector.tensor_copy(pa[:, t, :], ym[t][:].indirect(lists["n3"][:]))
-            nc.vector.tensor_copy(pb[:, t, :], ym[t][:].indirect(lists["n4"][:]))
-
-        st = planes("st", WIDE)
-        st_again = planes("st_again", S)
-
-        def pull(t):
-            nc.vector.tensor_tensor(st[t][:, :S], yh[t][:].indirect(lists["n1"][:]), yn[t][:], ALU.add)
-            nc.sync.dma_start(st_again[t][:], st[t][:, :S])
-
+            scaled_y(yh[t], t, gains[:, 0, t : t + 1])
+            scaled_y(yn[t], t, gains[:, 1, t : t + 1])
         lo = sb("lo", [P, PACK, S], BF16)
         hi = sb("hi", [P, PACK, S], BF16)
         mid = sb("mid", [P, PACK, S], BF16)
         z2 = sb("z2", [P, PACK, S], BF16)
-        nc.vector.tensor_tensor(hi[:], pa[:], pb[:], ALU.max)
-        nc.vector.tensor_tensor(lo[:], pa[:], pb[:], ALU.min)
-        nc.vector.tensor_tensor(mid[:], hi[:], ym16[:], ALU.min)
-        pull(0)
-        nc.vector.tensor_tensor(z2[:], lo[:], mid[:], ALU.max)
+        pairs = (slice(0, 2), slice(2, 4))
+
+        def fetch(t):
+            nc.vector.tensor_copy(pa[:, t, :], ym[t][:].indirect(lists["n3"][:]))
+            nc.vector.tensor_copy(pb[:, t, :], ym[t][:].indirect(lists["n4"][:]))
+
+        def clamp(ts):
+            nc.vector.tensor_tensor(hi[:, ts, :], pa[:, ts, :], pb[:, ts, :], ALU.max)
+            nc.vector.tensor_tensor(lo[:, ts, :], pa[:, ts, :], pb[:, ts, :], ALU.min)
+            nc.vector.tensor_tensor(mid[:, ts, :], hi[:, ts, :], ym16[:, ts, :], ALU.min)
+
+        for t in range(PACK):
+            fetch(t)
+        clamp(pairs[0])
+        deal_scales(w23s, w23s_raw)
+        clamp(pairs[1])
+        for ts in pairs:
+            nc.vector.tensor_tensor(z2[:, ts, :], lo[:, ts, :], mid[:, ts, :], ALU.max)
         z2_grouped = sb("z2_grouped", [P, PACK * S], BF16)
-        interleave(nc.scalar.copy, z2_grouped, z2[:])
-        for t in range(1, PACK):
-            pull(t)
+        interleave(nc.scalar.copy, z2_grouped[:], z2[:])
 
-
-        def hop(t):
-            nc.vector.tensor_tensor(z[:, t, :], st[t][:].indirect(lists["n2"][:]), st_again[t][:], ALU.subtract)
+        st = planes("st", WIDE)
+        st_again = planes("st_again", S)
+        for t in range(PACK):
+            nc.vector.tensor_tensor(st[t][:, :S], yh[t][:].indirect(lists["n1"][:]), yn[t][:], ALU.add)
+            if t < PACK - 1:
+                nc.sync.dma_start(st_again[t][:], st[t][:, :S])
+            else:
+                nc.scalar.copy(st_again[t][:], st[t][:, :S])
 
         z2_codes = sb("z2_codes", [P, S], I32)
         z2_plane = sb("z2_plane", [P, S], U8)
         nc.vector.quantize_mx(z2_codes[:].bitcast(FP8X4), z2_plane[:], z2_grouped[:])
-        z = sb("z", [P, PACK, S], F32, tag="z2_grouped")
         bw = planes("bw", WIDE)
         b_again = planes("b_again", S)
         for t in range(PACK):
-            product(b_ps[t], t, w3_dealt, w23s, 8, z2_codes, z2_plane)
+            product(b_ps[t][:], t, w3_dealt, w23s, 8, z2_codes[:], z2_plane[:])
         for t in range(PACK):
             nc.scalar.copy(bw[t][:, :S], b_ps[t][:])
             nc.sync.dma_start(b_again[t][:], bw[t][:, :S])
-        for t in range(PACK):
-            hop(t)
-        z_grouped = sb("z_grouped", [P, PACK * S], BF16)
-        interleave(nc.scalar.copy, z_grouped, z[:])
 
-        u = [sb("u%d" % t, [P, S], F32) for t in range(PACK - 1)]
+        z = sb("z", [P, len(HALVES), PACK, S // 2], F32, tag="z2_grouped")
+        z_grouped = sb("z_grouped", [P, PACK * S], BF16, tag="z2_codes")
+        for h, cols in enumerate(HALVES):
+            for t in range(PACK):
+                nc.vector.tensor_tensor(z[:, h, t, :], st[t][:].indirect(lists["n2"][:, entries(cols)]),
+                                        st_again[t][:, cols], ALU.subtract)
+            interleave(nc.scalar.copy, z_grouped[:, PACK * cols.start : PACK * cols.stop], z[:, h, :, :])
+
         gate = planes("gate", S)
 
-        def gating(t):
-            nc.vector.tensor_tensor(u[t][:], bw[t][:].indirect(lists["n6"][:]), b_again[t][:], ALU.subtract)
-            nc.scalar.activation(gate[t][:], u[t][:], ACT.Sigmoid)
+        def gating(u, ts):
+            for t in range(ts.start, ts.stop):
+                row = u[:, t - ts.start, :]
+                nc.vector.tensor_tensor(row, bw[t][:].indirect(lists["n6"][:]), b_again[t][:], ALU.subtract)
+                nc.scalar.activation(gate[t][:], row, ACT.Sigmoid)
 
-        for t in range(PACK - 1):
-            gating(t)
+        gating(sb("u_first", [P, 2, S], F32), pairs[0])
         z_codes = sb("z_codes", [P, S], I32)
         z_plane = sb("z_plane", [P, S], U8)
         nc.vector.quantize_mx(z_codes[:].bitcast(FP8X4), z_plane[:], z_grouped[:])
-        u.append(sb("u_last", [P, S], F32, tag="z_grouped"))
-        gating(PACK - 1)
+        gating(sb("u_second", [P, 2, S], F32, tag="z2_codes"), pairs[1])
         a_ps = y_ps
         for t in range(PACK):
-            product(a_ps[t], t, w2_dealt, w23s, 4, z_codes, z_plane)
+            product(a_ps[t][:], t, w2_dealt, w23s, 4, z_codes[:], z_plane[:])
         aw = planes("aw", S)
         own = sb("own", [P, PACK, S], F32)
         for t in range(PACK):
@@ -225,9 +249,9 @@ def tile_picked_forkpullbhopmed_none_po_kernel(
                     nc.vector.scalar_tensor_tensor(own[:, t, :], gate[t][:], 1.0, aw[t][:], ALU.subtract, ALU.mult)
             nc.vector.tensor_tensor(res[:], other[:], own[:, :, j0:j1], ALU.subtract)
             nc.sync.dma_start(out_rows[:, :, j0:j1], res[:])
-            interleave(nc.scalar.copy, res_grouped, res[:])
+            interleave(nc.scalar.copy, res_grouped[:], res[:])
             nc.vector.quantize_mx(res_codes[:].bitcast(FP8X4), out_plane[:, j0:j1], res_grouped[:])
             nc.sync.dma_start(out_words[:, j0:j1], res_codes[:])
         for q in range(4):
-            nc.sync.dma_start(out_2[0, 4 * q : 4 * q + 4, :].bitcast(I32),
+            (nc.sync, nc.scalar)[q % 2].dma_start(out_2[0, 4 * q : 4 * q + 4, :].bitcast(I32),
                               out_plane[32 * q : 32 * q + 4, :].bitcast(I32))

@@ -18,7 +18,8 @@ ACT = mybir.ActivationFunctionType
 P = 128
 PACK = 4
 WIDE = 2 * S
-CHUNKS = ((0, 128), (128, 256), (256, 384), (384, 512))
+LAST = 128
+EARLY, LATE = slice(0, S - LAST), slice(S - LAST, S)
 HALVES = (slice(0, S // 2), slice(S // 2, S))
 
 
@@ -37,7 +38,6 @@ def tile_picked_forkpullbhopmed_none_po_kernel(
     nc = tc.nc
     with ExitStack() as ctx:
         keep = ctx.enter_context(tc.tile_pool(name="keep", bufs=1))
-        ring = ctx.enter_context(tc.tile_pool(name="ring", bufs=2))
         psum = ctx.enter_context(tc.psum_pool(name="psum", bufs=1))
 
         def sb(name, shape, dtype, tag=None):
@@ -54,15 +54,16 @@ def tile_picked_forkpullbhopmed_none_po_kernel(
                 queue.dma_start(plane[32 * q + first : 32 * q + first + 4, :].bitcast(I32),
                                 scales[0, 4 * q : 4 * q + 4, :].bitcast(I32))
 
-        def deal_words(dealt, raw):
+        def deal(dealt, raw, run, ts):
             nc.vector.tensor_copy(
-                dealt[:].bitcast(U32).rearrange("p (t b i) -> p b t i", t=PACK, i=4),
-                raw[:].bitcast(U32).rearrange("p (b i t) -> p b t i", t=PACK, i=4))
+                dealt.rearrange("p (t b i) -> p b t i", t=PACK, i=run)[:, :, ts, :],
+                raw.rearrange("p (b i t) -> p b t i", t=PACK, i=run)[:, :, ts, :])
 
-        def deal_scales(dealt, raw):
-            nc.vector.tensor_copy(
-                dealt[:].rearrange("p (t b i) -> p b t i", t=PACK, i=16),
-                raw[:].rearrange("p (b i t) -> p b t i", t=PACK, i=16))
+        def deal_words(dealt, raw, ts=slice(0, PACK)):
+            deal(dealt[:].bitcast(U32), raw[:].bitcast(U32), 4, ts)
+
+        def deal_scales(dealt, raw, ts=slice(0, PACK)):
+            deal(dealt[:], raw[:], 16, ts)
 
         def interleave(engine_copy, grouped, by_plane):
             engine_copy(grouped.rearrange("p (c i t) -> p c t i", t=PACK, i=4),
@@ -91,15 +92,15 @@ def tile_picked_forkpullbhopmed_none_po_kernel(
         nc.scalar.activation(warm[:], warm[:], ACT.Sigmoid)
 
         nc.sync.dma_start(lists["offs"][:], offs)
-        nc.sync.dma_start(x_raw[:, : T // 2], words_of(x_words)[:, : T // 2])
+        nc.sync.dma_start(x_raw[:, : T // 4], words_of(x_words)[:, : T // 4])
         load_scale_rows(nc.sync, xs_raw, x_scales, 0)
-        nc.sync.dma_start(x_raw[:, T // 2 :], words_of(x_words)[:, T // 2 :])
+        nc.sync.dma_start(x_raw[:, T // 4 :], words_of(x_words)[:, T // 4 :])
         nc.sync.dma_start(w1_raw[:], words_of(w1_words))
         load_scale_rows(nc.sync, w1s_raw, w1_scales, 0)
-        nc.sync.dma_start(w3_raw[:], words_of(w3_words))
         nc.sync.dma_start(gm_sb[:], gm.rearrange("(p t) o -> p (t o)", t=PACK))
-        nc.sync.dma_start(lists["n3"][:], n3)
+        nc.sync.dma_start(w3_raw[:], words_of(w3_words))
         nc.sync.dma_start(w2_raw[:], words_of(w2_words))
+        nc.sync.dma_start(lists["n3"][:], n3)
         nc.sync.dma_start(lists["n4"][:], n4)
         nc.sync.dma_start(gn_sb[:], gn.rearrange("(p t) o -> p (t o)", t=PACK))
         load_scale_rows(nc.sync, w23s_raw, w3_scales, 8)
@@ -124,9 +125,11 @@ def tile_picked_forkpullbhopmed_none_po_kernel(
                                   x_raw[:].bitcast(U32).indirect(lists["offs"][:, entries(cols)]))
 
         pick_words(HALVES[0])
-        deal_words(w1_dealt, w1_raw)
-        deal_scales(w1s, w1s_raw)
+        deal_words(w1_dealt, w1_raw, slice(0, 1))
+        deal_scales(w1s, w1s_raw, slice(0, 1))
         pick_words(HALVES[1])
+        deal_words(w1_dealt, w1_raw, slice(1, PACK))
+        deal_scales(w1s, w1s_raw, slice(1, PACK))
 
         banks = [psum.tile([P, S], F32, name="bank%d" % b) for b in range(2 * PACK)]
         y_ps, b_ps = banks[:PACK], banks[PACK:]
@@ -141,8 +144,8 @@ def tile_picked_forkpullbhopmed_none_po_kernel(
                 nc.scalar.activation(row[:, cols], result, ACT.Copy, scale=gain)
 
         gains = sb("gains", [P, 2, PACK], F32)
-        nc.vector.tensor_scalar(gains[:, 0, :], gn_sb[:], -0.5, None, ALU.mult)
-        nc.vector.tensor_scalar(gains[:, 1, :], gn_sb[:], -1.0, None, ALU.mult)
+        nc.scalar.mul(gains[:, 0, :], gn_sb[:], -0.5)
+        nc.scalar.mul(gains[:, 1, :], gn_sb[:], -1.0)
         deal_words(w3_dealt, w3_raw)
         deal_words(w2_dealt, w2_raw)
 
@@ -165,33 +168,29 @@ def tile_picked_forkpullbhopmed_none_po_kernel(
         z2 = sb("z2", [P, PACK, S], BF16)
         pairs = (slice(0, 2), slice(2, 4))
 
-        def fetch(t):
-            nc.vector.tensor_copy(pa[:, t, :], ym[t][:].indirect(lists["n3"][:]))
-            nc.vector.tensor_copy(pb[:, t, :], ym[t][:].indirect(lists["n4"][:]))
-
-        def clamp(ts):
-            nc.vector.tensor_tensor(hi[:, ts, :], pa[:, ts, :], pb[:, ts, :], ALU.max)
-            nc.vector.tensor_tensor(lo[:, ts, :], pa[:, ts, :], pb[:, ts, :], ALU.min)
-            nc.vector.tensor_tensor(mid[:, ts, :], hi[:, ts, :], ym16[:, ts, :], ALU.min)
-
-        for t in range(PACK):
-            fetch(t)
-        clamp(pairs[0])
-        deal_scales(w23s, w23s_raw)
-        clamp(pairs[1])
-        for ts in pairs:
-            nc.vector.tensor_tensor(z2[:, ts, :], lo[:, ts, :], mid[:, ts, :], ALU.max)
-        z2_grouped = sb("z2_grouped", [P, PACK * S], BF16)
-        interleave(nc.scalar.copy, z2_grouped[:], z2[:])
-
         st = planes("st", WIDE)
         st_again = planes("st_again", S)
-        for t in range(PACK):
+
+        def pull(t):
             nc.vector.tensor_tensor(st[t][:, :S], yh[t][:].indirect(lists["n1"][:]), yn[t][:], ALU.add)
             if t < PACK - 1:
                 nc.sync.dma_start(st_again[t][:], st[t][:, :S])
             else:
                 nc.scalar.copy(st_again[t][:], st[t][:, :S])
+
+        for t in range(PACK):
+            nc.vector.tensor_copy(pa[:, t, :], ym[t][:].indirect(lists["n3"][:]))
+            nc.vector.tensor_copy(pb[:, t, :], ym[t][:].indirect(lists["n4"][:]))
+        deal_scales(w23s, w23s_raw)
+        nc.vector.tensor_tensor(hi[:], pa[:], pb[:], ALU.max)
+        nc.vector.tensor_tensor(lo[:], pa[:], pb[:], ALU.min)
+        nc.vector.tensor_tensor(mid[:], hi[:], ym16[:], ALU.min)
+        pull(0)
+        nc.vector.tensor_tensor(z2[:], lo[:], mid[:], ALU.max)
+        z2_grouped = sb("z2_grouped", [P, PACK * S], BF16)
+        interleave(nc.scalar.copy, z2_grouped[:], z2[:])
+        for t in range(1, PACK):
+            pull(t)
 
         z2_codes = sb("z2_codes", [P, S], I32)
         z2_plane = sb("z2_plane", [P, S], U8)
@@ -204,13 +203,18 @@ def tile_picked_forkpullbhopmed_none_po_kernel(
             nc.scalar.copy(bw[t][:, :S], b_ps[t][:])
             nc.sync.dma_start(b_again[t][:], bw[t][:, :S])
 
-        z = sb("z", [P, len(HALVES), PACK, S // 2], F32, tag="z2_grouped")
+        z = sb("z", [P, PACK, S], F32, tag="z2_grouped")
         z_grouped = sb("z_grouped", [P, PACK * S], BF16, tag="z2_codes")
-        for h, cols in enumerate(HALVES):
-            for t in range(PACK):
-                nc.vector.tensor_tensor(z[:, h, t, :], st[t][:].indirect(lists["n2"][:, entries(cols)]),
-                                        st_again[t][:, cols], ALU.subtract)
-            interleave(nc.scalar.copy, z_grouped[:, PACK * cols.start : PACK * cols.stop], z[:, h, :, :])
+
+        def hop(t, cols):
+            nc.vector.tensor_tensor(z[:, t, cols], st[t][:].indirect(lists["n2"][:, entries(cols)]),
+                                    st_again[t][:, cols], ALU.subtract)
+
+        for t in (0, PACK - 1, 1):
+            hop(t, slice(0, S))
+        for cols in HALVES:
+            hop(2, cols)
+            interleave(nc.scalar.copy, z_grouped[:, PACK * cols.start : PACK * cols.stop], z[:, :, cols])
 
         gate = planes("gate", S)
 
@@ -235,23 +239,52 @@ def tile_picked_forkpullbhopmed_none_po_kernel(
 
         out_rows = out_0.rearrange("(p t) j -> p t j", t=PACK)
         out_words = words_of(out_1)
-        out_plane = sb("out_plane", [P, S], U8)
-        for c, (j0, j1) in enumerate(CHUNKS):
-            width = j1 - j0
-            other = ring.tile([P, PACK, width], F32, name="other")
-            res = sb("res%d" % c, [P, PACK, width], F32)
-            res_grouped = sb("res_grouped%d" % c, [P, PACK * width], BF16)
-            res_codes = sb("res_codes%d" % c, [P, width], I32)
-            for t in range(PACK):
-                nc.vector.tensor_tensor(other[:, t, :], aw[t][:].indirect(lists["n5"][:, j0 // 16 : j1 // 16]),
-                                        gate[t][:, j0:j1], ALU.mult)
-                if c == 0:
-                    nc.vector.scalar_tensor_tensor(own[:, t, :], gate[t][:], 1.0, aw[t][:], ALU.subtract, ALU.mult)
-            nc.vector.tensor_tensor(res[:], other[:], own[:, :, j0:j1], ALU.subtract)
-            nc.sync.dma_start(out_rows[:, :, j0:j1], res[:])
-            interleave(nc.scalar.copy, res_grouped[:], res[:])
-            nc.vector.quantize_mx(res_codes[:].bitcast(FP8X4), out_plane[:, j0:j1], res_grouped[:])
-            nc.sync.dma_start(out_words[:, j0:j1], res_codes[:])
+        res_codes = sb("res_codes", [P, S], I32)
+        res_plane = sb("res_plane", [P, S], U8)
+        res_grouped = sb("res_grouped", [P, PACK * S], BF16)
+
+        def fetch_a(other, t, cols):
+            nc.vector.tensor_tensor(other, aw[t][:].indirect(lists["n5"][:, entries(cols)]), gate[t][:, cols], ALU.mult)
+
+        def to_planes(res, cols):
+            grouped = res_grouped[:, PACK * cols.start : PACK * cols.stop]
+            interleave(nc.scalar.copy, grouped, res)
+            nc.vector.quantize_mx(res_codes[:, cols].bitcast(FP8X4), res_plane[:, cols], grouped)
+
+        other_early = planes("other_early", S - LAST)
+        res_early = sb("res_early", [P, PACK, S - LAST], F32)
+
+        def join_early(t):
+            nc.vector.tensor_tensor(res_early[:, t, :], other_early[t][:], own[:, t, EARLY], ALU.subtract)
+            nc.sync.dma_start(out_rows[:, t, EARLY], res_early[:, t, :])
+
+        for t in range(PACK):
+            nc.vector.scalar_tensor_tensor(own[:, t, :], gate[t][:], 1.0, aw[t][:], ALU.subtract, ALU.mult)
+            fetch_a(other_early[t][:], t, EARLY)
+            if t > 0:
+                join_early(t - 1)
+        join_early(PACK - 1)
+
+        other_late = sb("other_late", [P, PACK, LAST], F32, tag="other_early%d" % (PACK - 2))
+        res_late = sb("res_late", [P, PACK, LAST], F32)
+
+        def join_late(ts):
+            nc.vector.tensor_tensor(res_late[:, ts, :], other_late[:, ts, :], own[:, ts, LATE], ALU.subtract)
+            nc.sync.dma_start(out_rows[:, ts, LATE], res_late[:, ts, :])
+
+        for t in range(PACK - 1):
+            fetch_a(other_late[:, t, :], t, LATE)
+        join_late(pairs[0])
+        fetch_a(other_late[:, PACK - 1, :], PACK - 1, LATE)
+        for cols in (HALVES[0], slice(S // 2, S - LAST)):
+            to_planes(res_early[:, :, cols], cols)
+        nc.sync.dma_start(out_words[:, EARLY], res_codes[:, EARLY])
+        join_late(pairs[1])
+        for copy, j0 in ((nc.scalar.copy, 0), (nc.vector.tensor_copy, LAST // 2)):
+            interleave(copy, res_grouped[:, PACK * (LATE.start + j0) : PACK * (LATE.start + j0 + LAST // 2)],
+                       res_late[:, :, j0 : j0 + LAST // 2])
+        nc.vector.quantize_mx(res_codes[:, LATE].bitcast(FP8X4), res_plane[:, LATE], res_grouped[:, PACK * LATE.start :])
+        nc.sync.dma_start(out_words[:, LATE], res_codes[:, LATE])
         for q in range(4):
             (nc.sync, nc.scalar)[q % 2].dma_start(out_2[0, 4 * q : 4 * q + 4, :].bitcast(I32),
-                              out_plane[32 * q : 32 * q + 4, :].bitcast(I32))
+                                                  res_plane[32 * q : 32 * q + 4, :].bitcast(I32))

@@ -1,6 +1,7 @@
 from contextlib import ExitStack
 
 import concourse.mybir as mybir
+from concourse.masks import make_identity
 
 K, T, S, N, H = 512, 2048, 512, 512, 512
 FLOPS = 2 * K * H * S + 2 * 2 * H * N * S
@@ -91,6 +92,9 @@ def tile_picked_forkpullbhopmed_none_po_kernel(
         nc.vector.memset(warm[:], 0.0)
         nc.scalar.activation(warm[:], warm[:], ACT.Sigmoid)
 
+        identity = sb("identity", [P, P], F32)
+        make_identity(nc, identity[:])
+
         nc.sync.dma_start(lists["offs"][:], offs)
         nc.sync.dma_start(x_raw[:, : T // 4], words_of(x_words)[:, : T // 4])
         load_scale_rows(nc.sync, xs_raw, x_scales, 0)
@@ -120,15 +124,9 @@ def tile_picked_forkpullbhopmed_none_po_kernel(
 
         nc.vector.tensor_copy(x_plane[:], xs_raw[:].indirect(lists["offs"][:]))
 
-        def pick_words(cols):
-            nc.vector.tensor_copy(x_codes[:, cols].bitcast(U32),
-                                  x_raw[:].bitcast(U32).indirect(lists["offs"][:, entries(cols)]))
-
-        pick_words(HALVES[0])
-        deal_words(w1_dealt, w1_raw, slice(0, 1))
+        nc.vector.tensor_copy(x_codes[:].bitcast(U32), x_raw[:].bitcast(U32).indirect(lists["offs"][:]))
+        deal_words(w1_dealt, w1_raw)
         deal_scales(w1s, w1s_raw, slice(0, 1))
-        pick_words(HALVES[1])
-        deal_words(w1_dealt, w1_raw, slice(1, PACK))
         deal_scales(w1s, w1s_raw, slice(1, PACK))
 
         banks = [psum.tile([P, S], F32, name="bank%d" % b) for b in range(2 * PACK)]
@@ -218,24 +216,34 @@ def tile_picked_forkpullbhopmed_none_po_kernel(
 
         gate = planes("gate", S)
 
-        def gating(u, ts):
+        def differences(u, ts):
             for t in range(ts.start, ts.stop):
-                row = u[:, t - ts.start, :]
-                nc.vector.tensor_tensor(row, bw[t][:].indirect(lists["n6"][:]), b_again[t][:], ALU.subtract)
-                nc.scalar.activation(gate[t][:], row, ACT.Sigmoid)
+                nc.vector.tensor_tensor(u[:, t - ts.start, :], bw[t][:].indirect(lists["n6"][:]), b_again[t][:],
+                                        ALU.subtract)
 
-        gating(sb("u_first", [P, 2, S], F32), pairs[0])
+        def gates(u, ts):
+            for t in range(ts.start, ts.stop):
+                nc.scalar.activation(gate[t][:], u[:, t - ts.start, :], ACT.Sigmoid)
+
+        u_first = sb("u_first", [P, 2, S], F32)
+        differences(u_first, pairs[0])
+        gates(u_first, pairs[0])
         z_codes = sb("z_codes", [P, S], I32)
         z_plane = sb("z_plane", [P, S], U8)
         nc.vector.quantize_mx(z_codes[:].bitcast(FP8X4), z_plane[:], z_grouped[:])
-        gating(sb("u_second", [P, 2, S], F32, tag="z2_codes"), pairs[1])
+        u_second = sb("u_second", [P, 2, S], F32, tag="z2_codes")
+        differences(u_second, pairs[1])
         a_ps = y_ps
         for t in range(PACK):
             product(a_ps[t][:], t, w2_dealt, w23s, 4, z_codes[:], z_plane[:])
-        aw = planes("aw", S)
+        aw = [sb("aw%d" % t, [P, WIDE if t < 2 else S], F32) for t in range(PACK)]
         own = sb("own", [P, PACK, S], F32)
+        keep_own = sb("keep_own", [P, 2, S], F32)
         for t in range(PACK):
-            nc.scalar.copy(aw[t][:], a_ps[t][:])
+            if t < 2:
+                nc.scalar.activation(keep_own[:, t, :], u_first[:, t, :], ACT.Sigmoid, scale=-1.0)
+            nc.scalar.copy(aw[t][:, :S], a_ps[t][:])
+        gates(u_second, pairs[1])
 
         out_rows = out_0.rearrange("(p t) j -> p t j", t=PACK)
         out_words = words_of(out_1)
@@ -246,44 +254,61 @@ def tile_picked_forkpullbhopmed_none_po_kernel(
         def fetch_a(other, t, cols):
             nc.vector.tensor_tensor(other, aw[t][:].indirect(lists["n5"][:, entries(cols)]), gate[t][:, cols], ALU.mult)
 
-        def to_planes(res, cols):
-            grouped = res_grouped[:, PACK * cols.start : PACK * cols.stop]
-            interleave(nc.scalar.copy, grouped, res)
-            nc.vector.quantize_mx(res_codes[:, cols].bitcast(FP8X4), res_plane[:, cols], grouped)
+        def group(copy, res, cols):
+            interleave(copy, res_grouped[:, PACK * cols.start : PACK * cols.stop], res)
 
-        other_early = planes("other_early", S - LAST)
+        def quantise(cols):
+            nc.vector.quantize_mx(res_codes[:, cols].bitcast(FP8X4), res_plane[:, cols],
+                                  res_grouped[:, PACK * cols.start : PACK * cols.stop])
+
         res_early = sb("res_early", [P, PACK, S - LAST], F32)
+        res_late = sb("res_late", [P, PACK, LAST], F32)
+        blocks = [slice(j, j + P) for j in range(0, S, P)]
+
+        for t in range(2):
+            other = sb("other%d" % t, [P, S], F32)
+            turned = sb("turned%d" % t, [P, S], F32)
+            nc.vector.tensor_tensor(own[:, t, :], keep_own[:, t, :], aw[t][:, :S], ALU.mult)
+            fetch_a(other[:], t, slice(0, S))
+            sum_ps, back_ps = b_ps[2 * t], b_ps[2 * t + 1]
+            for cols in blocks:
+                terms = (own[:, t, cols], other[:, cols])
+                for i, term in enumerate(terms):
+                    nc.tensor.matmul(sum_ps[:, cols], term, identity[:], start=i == 0, stop=i == len(terms) - 1,
+                                     is_transpose=True)
+            nc.scalar.copy(turned[:], sum_ps[:])
+            for cols in blocks:
+                nc.tensor.transpose(back_ps[:, cols], turned[:, cols], identity[:])
+            nc.scalar.copy(res_early[:, t, :], back_ps[:, EARLY])
+            nc.scalar.copy(res_late[:, t, :], back_ps[:, LATE])
+        nc.sync.dma_start(out_rows[:, 0, EARLY], res_early[:, 0, :])
+
+        other_early = {t: sb("other_early%d" % t, [P, S - LAST], F32) for t in (2, 3)}
 
         def join_early(t):
             nc.vector.tensor_tensor(res_early[:, t, :], other_early[t][:], own[:, t, EARLY], ALU.subtract)
-            nc.sync.dma_start(out_rows[:, t, EARLY], res_early[:, t, :])
 
-        for t in range(PACK):
-            nc.vector.scalar_tensor_tensor(own[:, t, :], gate[t][:], 1.0, aw[t][:], ALU.subtract, ALU.mult)
-            fetch_a(other_early[t][:], t, EARLY)
-            if t > 0:
-                join_early(t - 1)
-        join_early(PACK - 1)
+        nc.vector.scalar_tensor_tensor(own[:, 2, :], gate[2][:], 1.0, aw[2][:], ALU.subtract, ALU.mult)
+        fetch_a(other_early[2][:], 2, EARLY)
+        nc.vector.scalar_tensor_tensor(own[:, 3, :], gate[3][:], 1.0, aw[3][:], ALU.subtract, ALU.mult)
+        fetch_a(other_early[3][:], 3, EARLY)
+        join_early(2)
+        join_early(3)
+        nc.sync.dma_start(out_rows[:, 1:, EARLY], res_early[:, 1:, :])
+        group(nc.scalar.copy, res_early[:, :, HALVES[0]], HALVES[0])
 
-        other_late = sb("other_late", [P, PACK, LAST], F32, tag="other_early%d" % (PACK - 2))
-        res_late = sb("res_late", [P, PACK, LAST], F32)
-
-        def join_late(ts):
-            nc.vector.tensor_tensor(res_late[:, ts, :], other_late[:, ts, :], own[:, ts, LATE], ALU.subtract)
-            nc.sync.dma_start(out_rows[:, ts, LATE], res_late[:, ts, :])
-
-        for t in range(PACK - 1):
-            fetch_a(other_late[:, t, :], t, LATE)
-        join_late(pairs[0])
-        fetch_a(other_late[:, PACK - 1, :], PACK - 1, LATE)
-        for cols in (HALVES[0], slice(S // 2, S - LAST)):
-            to_planes(res_early[:, :, cols], cols)
+        other_late = sb("other_late", [P, 2, LAST], F32, tag="other_early2")
+        for t in (2, 3):
+            fetch_a(other_late[:, t - 2, :], t, LATE)
+        third = slice(S // 2, S - LAST)
+        group(nc.vector.tensor_copy, res_early[:, :, third], third)
+        nc.vector.tensor_tensor(res_late[:, pairs[1], :], other_late[:], own[:, pairs[1], LATE], ALU.subtract)
+        nc.sync.dma_start(out_rows[:, :, LATE], res_late[:])
+        quantise(third)
+        group(nc.vector.tensor_copy, res_late[:], LATE)
+        quantise(HALVES[0])
         nc.sync.dma_start(out_words[:, EARLY], res_codes[:, EARLY])
-        join_late(pairs[1])
-        for copy, j0 in ((nc.scalar.copy, 0), (nc.vector.tensor_copy, LAST // 2)):
-            interleave(copy, res_grouped[:, PACK * (LATE.start + j0) : PACK * (LATE.start + j0 + LAST // 2)],
-                       res_late[:, :, j0 : j0 + LAST // 2])
-        nc.vector.quantize_mx(res_codes[:, LATE].bitcast(FP8X4), res_plane[:, LATE], res_grouped[:, PACK * LATE.start :])
+        quantise(LATE)
         nc.sync.dma_start(out_words[:, LATE], res_codes[:, LATE])
         for q in range(4):
             (nc.sync, nc.scalar)[q % 2].dma_start(out_2[0, 4 * q : 4 * q + 4, :].bitcast(I32),

from contextlib import ExitStack

import concourse.mybir as mybir
from concourse.masks import make_identity

K, T, S, N, H = 512, 2048, 512, 512, 512
FLOPS = 2 * K * H * S + 2 * 2 * H * N * S

F32 = mybir.dt.float32
BF16 = mybir.dt.bfloat16
I32 = mybir.dt.int32
U32 = mybir.dt.uint32
U16 = mybir.dt.uint16
U8 = mybir.dt.uint8
FP8X4 = mybir.dt.float8_e4m3fn_x4
ALU = mybir.AluOpType
ACT = mybir.ActivationFunctionType

P = 128
PACK = 4
WIDE = 2 * S
LAST = 128
EARLY, LATE = slice(0, S - LAST), slice(S - LAST, S)
HALVES = (slice(0, S // 2), slice(S // 2, S))


def entries(cols):
    return slice(cols.start // 16, cols.stop // 16)


def words_of(packed):
    return packed[0].rearrange("p n t -> p (n t)").bitcast(I32)


def tile_picked_forkpullbhopmed_none_po_kernel(
    tc, x_words, x_scales, w1_words, w1_scales, gn, w2_words, w2_scales, gm, w3_words, w3_scales,
    offs, n1, n2, n3, n4, n5, n6, out_0, out_1, out_2,
):
    nc = tc.nc
    with ExitStack() as ctx:
        keep = ctx.enter_context(tc.tile_pool(name="keep", bufs=1))
        psum = ctx.enter_context(tc.psum_pool(name="psum", bufs=1))

        def sb(name, shape, dtype, tag=None):
            return keep.tile(shape, dtype, name=name, tag=tag or name, align_bytes=64)

        def planes(name, width, dtype=F32):
            return [sb("%s%d" % (name, t), [P, width], dtype) for t in range(PACK)]

        lists = {name: keep.tile([P, S // 16], U16, name="list_" + name)
                 for name in ("offs", "n1", "n2", "n3", "n4", "n5", "n6")}

        def load_scale_rows(queue, plane, scales, first):
            for q in range(4):
                queue.dma_start(plane[32 * q + first : 32 * q + first + 4, :].bitcast(I32),
                                scales[0, 4 * q : 4 * q + 4, :].bitcast(I32))

        def deal(dealt, raw, run, ts):
            nc.vector.tensor_copy(
                dealt.rearrange("p (t b i) -> p b t i", t=PACK, i=run)[:, :, ts, :],
                raw.rearrange("p (b i t) -> p b t i", t=PACK, i=run)[:, :, ts, :])

        def deal_words(dealt, raw, ts=slice(0, PACK)):
            deal(dealt[:].bitcast(U32), raw[:].bitcast(U32), 4, ts)

        def deal_scales(dealt, raw, ts=slice(0, PACK)):
            deal(dealt[:], raw[:], 16, ts)

        def interleave(engine_copy, grouped, by_plane):
            engine_copy(grouped.rearrange("p (c i t) -> p c t i", t=PACK, i=4),
                        by_plane.rearrange("p t (c i) -> p c t i", i=4))

        def product(result, t, w_dealt, w_plane, first, codes, scales):
            cols = slice(t * P, (t + 1) * P)
            nc.tensor.matmul_mx(result, lhsT=w_dealt[:, cols].bitcast(FP8X4), lhsT_scale=w_plane[first:, cols],
                                rhs=codes.bitcast(FP8X4), rhs_scale=scales, start=True, stop=True)

        x_raw = sb("x_raw", [P, T], I32)
        xs_raw = sb("xs_raw", [P, T], U8)
        w1_raw = sb("w1_raw", [P, H], I32)
        w2_raw = sb("w2_raw", [P, N], I32)
        w3_raw = sb("w3_raw", [P, N], I32)
        w1s_raw = sb("w1s_raw", [P, H], U8)
        w23s_raw = sb("w23s_raw", [P, N], U8)
        gn_sb = sb("gn_sb", [P, PACK], F32)
        gm_sb = sb("gm_sb", [P, PACK], F32)
        warm = sb("warm", [P, 1], F32)

        nc.vector.memset(xs_raw[:].bitcast(I32), 0)
        nc.vector.memset(w1s_raw[:].bitcast(I32), 0)
        nc.vector.memset(w23s_raw[:].bitcast(I32), 0)
        nc.vector.memset(warm[:], 0.0)
        nc.scalar.activation(warm[:], warm[:], ACT.Sigmoid)

        identity = sb("identity", [P, P], F32)
        make_identity(nc, identity[:])

        nc.sync.dma_start(lists["offs"][:], offs)
        nc.sync.dma_start(x_raw[:, : T // 4], words_of(x_words)[:, : T // 4])
        load_scale_rows(nc.sync, xs_raw, x_scales, 0)
        nc.sync.dma_start(x_raw[:, T // 4 :], words_of(x_words)[:, T // 4 :])
        nc.sync.dma_start(w1_raw[:], words_of(w1_words))
        load_scale_rows(nc.sync, w1s_raw, w1_scales, 0)
        nc.sync.dma_start(gm_sb[:], gm.rearrange("(p t) o -> p (t o)", t=PACK))
        nc.sync.dma_start(w3_raw[:], words_of(w3_words))
        nc.sync.dma_start(w2_raw[:], words_of(w2_words))
        nc.sync.dma_start(lists["n3"][:], n3)
        nc.sync.dma_start(lists["n4"][:], n4)
        nc.sync.dma_start(gn_sb[:], gn.rearrange("(p t) o -> p (t o)", t=PACK))
        load_scale_rows(nc.sync, w23s_raw, w3_scales, 8)
        load_scale_rows(nc.sync, w23s_raw, w2_scales, 4)
        nc.sync.dma_start(lists["n1"][:], n1)
        nc.sync.dma_start(lists["n2"][:], n2)
        nc.sync.dma_start(lists["n6"][:], n6)
        nc.sync.dma_start(lists["n5"][:], n5)

        w1_dealt = sb("w1_dealt", [P, H], I32)
        w2_dealt = sb("w2_dealt", [P, N], I32)
        w3_dealt = sb("w3_dealt", [P, N], I32)
        w1s = sb("w1s", [P, H], U8)
        w23s = sb("w23s", [P, N], U8)
        x_codes = sb("x_codes", [P, S], I32)
        x_plane = sb("x_plane", [P, S], U8)

        nc.vector.tensor_copy(x_plane[:], xs_raw[:].indirect(lists["offs"][:]))

        nc.vector.tensor_copy(x_codes[:].bitcast(U32), x_raw[:].bitcast(U32).indirect(lists["offs"][:]))
        deal_words(w1_dealt, w1_raw)
        deal_scales(w1s, w1s_raw, slice(0, 1))
        deal_scales(w1s, w1s_raw, slice(1, PACK))

        banks = [psum.tile([P, S], F32, name="bank%d" % b) for b in range(2 * PACK)]
        y_ps, b_ps = banks[:PACK], banks[PACK:]
        y_parts = [[(cols, bank[:, cols]) for cols, bank in zip(HALVES, (y_ps[0], b_ps[0]))]]
        y_parts.extend([(slice(0, S), y_ps[t][:])] for t in range(1, PACK))
        for t in range(PACK):
            for cols, result in y_parts[t]:
                product(result, t, w1_dealt, w1s, 0, x_codes[:, cols], x_plane[:, cols])

        def scaled_y(row, t, gain):
            for cols, result in y_parts[t]:
                nc.scalar.activation(row[:, cols], result, ACT.Copy, scale=gain)

        gains = sb("gains", [P, 2, PACK], F32)
        nc.scalar.mul(gains[:, 0, :], gn_sb[:], -0.5)
        nc.scalar.mul(gains[:, 1, :], gn_sb[:], -1.0)
        deal_words(w3_dealt, w3_raw)
        deal_words(w2_dealt, w2_raw)

        ym = planes("ym", WIDE)
        ym16 = sb("ym16", [P, PACK, S], BF16)
        pa = sb("pa", [P, PACK, S], BF16)
        pb = sb("pb", [P, PACK, S], BF16)
        for t in range(PACK):
            scaled_y(ym[t], t, gm_sb[:, t : t + 1])
        yh = planes("yh", WIDE)
        yn = planes("yn", S)
        for t in range(PACK):
            scaled_y(ym16[:, t, :], t, gm_sb[:, t : t + 1])
        for t in range(PACK):
            scaled_y(yh[t], t, gains[:, 0, t : t + 1])
            scaled_y(yn[t], t, gains[:, 1, t : t + 1])
        lo = sb("lo", [P, PACK, S], BF16)
        hi = sb("hi", [P, PACK, S], BF16)
        mid = sb("mid", [P, PACK, S], BF16)
        z2 = sb("z2", [P, PACK, S], BF16)
        pairs = (slice(0, 2), slice(2, 4))

        st = planes("st", WIDE)
        st_again = planes("st_again", S)

        def pull(t):
            nc.vector.tensor_tensor(st[t][:, :S], yh[t][:].indirect(lists["n1"][:]), yn[t][:], ALU.add)
            if t < PACK - 1:
                nc.sync.dma_start(st_again[t][:], st[t][:, :S])
            else:
                nc.scalar.copy(st_again[t][:], st[t][:, :S])

        for t in range(PACK):
            nc.vector.tensor_copy(pa[:, t, :], ym[t][:].indirect(lists["n3"][:]))
            nc.vector.tensor_copy(pb[:, t, :], ym[t][:].indirect(lists["n4"][:]))
        deal_scales(w23s, w23s_raw)
        nc.vector.tensor_tensor(hi[:], pa[:], pb[:], ALU.max)
        nc.vector.tensor_tensor(lo[:], pa[:], pb[:], ALU.min)
        nc.vector.tensor_tensor(mid[:], hi[:], ym16[:], ALU.min)
        pull(0)
        nc.vector.tensor_tensor(z2[:], lo[:], mid[:], ALU.max)
        z2_grouped = sb("z2_grouped", [P, PACK * S], BF16)
        interleave(nc.scalar.copy, z2_grouped[:], z2[:])
        for t in range(1, PACK):
            pull(t)

        z2_codes = sb("z2_codes", [P, S], I32)
        z2_plane = sb("z2_plane", [P, S], U8)
        nc.vector.quantize_mx(z2_codes[:].bitcast(FP8X4), z2_plane[:], z2_grouped[:])
        bw = planes("bw", WIDE)
        b_again = planes("b_again", S)
        for t in range(PACK):
            product(b_ps[t][:], t, w3_dealt, w23s, 8, z2_codes[:], z2_plane[:])
        for t in range(PACK):
            nc.scalar.copy(bw[t][:, :S], b_ps[t][:])
            nc.sync.dma_start(b_again[t][:], bw[t][:, :S])

        z = sb("z", [P, PACK, S], F32, tag="z2_grouped")
        z_grouped = sb("z_grouped", [P, PACK * S], BF16, tag="z2_codes")

        def hop(t, cols):
            nc.vector.tensor_tensor(z[:, t, cols], st[t][:].indirect(lists["n2"][:, entries(cols)]),
                                    st_again[t][:, cols], ALU.subtract)

        for t in (0, PACK - 1, 1):
            hop(t, slice(0, S))
        for cols in HALVES:
            hop(2, cols)
            interleave(nc.scalar.copy, z_grouped[:, PACK * cols.start : PACK * cols.stop], z[:, :, cols])

        gate = planes("gate", S)

        def differences(u, ts):
            for t in range(ts.start, ts.stop):
                nc.vector.tensor_tensor(u[:, t - ts.start, :], bw[t][:].indirect(lists["n6"][:]), b_again[t][:],
                                        ALU.subtract)

        def gates(u, ts):
            for t in range(ts.start, ts.stop):
                nc.scalar.activation(gate[t][:], u[:, t - ts.start, :], ACT.Sigmoid)

        u_first = sb("u_first", [P, 2, S], F32)
        differences(u_first, pairs[0])
        gates(u_first, pairs[0])
        z_codes = sb("z_codes", [P, S], I32)
        z_plane = sb("z_plane", [P, S], U8)
        nc.vector.quantize_mx(z_codes[:].bitcast(FP8X4), z_plane[:], z_grouped[:])
        u_second = sb("u_second", [P, 2, S], F32, tag="z2_codes")
        differences(u_second, pairs[1])
        a_ps = y_ps
        for t in range(PACK):
            product(a_ps[t][:], t, w2_dealt, w23s, 4, z_codes[:], z_plane[:])
        aw = [sb("aw%d" % t, [P, WIDE if t < 2 else S], F32) for t in range(PACK)]
        own = sb("own", [P, PACK, S], F32)
        keep_own = sb("keep_own", [P, 2, S], F32)
        for t in range(PACK):
            if t < 2:
                nc.scalar.activation(keep_own[:, t, :], u_first[:, t, :], ACT.Sigmoid, scale=-1.0)
            nc.scalar.copy(aw[t][:, :S], a_ps[t][:])
        gates(u_second, pairs[1])

        out_rows = out_0.rearrange("(p t) j -> p t j", t=PACK)
        out_words = words_of(out_1)
        res_codes = sb("res_codes", [P, S], I32)
        res_plane = sb("res_plane", [P, S], U8)
        res_grouped = sb("res_grouped", [P, PACK * S], BF16)

        def fetch_a(other, t, cols):
            nc.vector.tensor_tensor(other, aw[t][:].indirect(lists["n5"][:, entries(cols)]), gate[t][:, cols], ALU.mult)

        def group(copy, res, cols):
            interleave(copy, res_grouped[:, PACK * cols.start : PACK * cols.stop], res)

        def quantise(cols):
            nc.vector.quantize_mx(res_codes[:, cols].bitcast(FP8X4), res_plane[:, cols],
                                  res_grouped[:, PACK * cols.start : PACK * cols.stop])

        res_early = sb("res_early", [P, PACK, S - LAST], F32)
        res_late = sb("res_late", [P, PACK, LAST], F32)
        blocks = [slice(j, j + P) for j in range(0, S, P)]

        for t in range(2):
            other = sb("other%d" % t, [P, S], F32)
            turned = sb("turned%d" % t, [P, S], F32)
            nc.vector.tensor_tensor(own[:, t, :], keep_own[:, t, :], aw[t][:, :S], ALU.mult)
            fetch_a(other[:], t, slice(0, S))
            sum_ps, back_ps = b_ps[2 * t], b_ps[2 * t + 1]
            for cols in blocks:
                terms = (own[:, t, cols], other[:, cols])
                for i, term in enumerate(terms):
                    nc.tensor.matmul(sum_ps[:, cols], term, identity[:], start=i == 0, stop=i == len(terms) - 1,
                                     is_transpose=True)
            nc.scalar.copy(turned[:], sum_ps[:])
            for cols in blocks:
                nc.tensor.transpose(back_ps[:, cols], turned[:, cols], identity[:])
            nc.scalar.copy(res_early[:, t, :], back_ps[:, EARLY])
            nc.scalar.copy(res_late[:, t, :], back_ps[:, LATE])
        nc.sync.dma_start(out_rows[:, 0, EARLY], res_early[:, 0, :])

        other_early = {t: sb("other_early%d" % t, [P, S - LAST], F32) for t in (2, 3)}

        def join_early(t):
            nc.vector.tensor_tensor(res_early[:, t, :], other_early[t][:], own[:, t, EARLY], ALU.subtract)

        nc.vector.scalar_tensor_tensor(own[:, 2, :], gate[2][:], 1.0, aw[2][:], ALU.subtract, ALU.mult)
        fetch_a(other_early[2][:], 2, EARLY)
        nc.vector.scalar_tensor_tensor(own[:, 3, :], gate[3][:], 1.0, aw[3][:], ALU.subtract, ALU.mult)
        fetch_a(other_early[3][:], 3, EARLY)
        join_early(2)
        join_early(3)
        nc.sync.dma_start(out_rows[:, 1:, EARLY], res_early[:, 1:, :])
        group(nc.scalar.copy, res_early[:, :, HALVES[0]], HALVES[0])

        other_late = sb("other_late", [P, 2, LAST], F32, tag="other_early2")
        for t in (2, 3):
            fetch_a(other_late[:, t - 2, :], t, LATE)
        third = slice(S // 2, S - LAST)
        group(nc.vector.tensor_copy, res_early[:, :, third], third)
        nc.vector.tensor_tensor(res_late[:, pairs[1], :], other_late[:], own[:, pairs[1], LATE], ALU.subtract)
        nc.sync.dma_start(out_rows[:, :, LATE], res_late[:])
        quantise(third)
        group(nc.vector.tensor_copy, res_late[:], LATE)
        quantise(HALVES[0])
        nc.sync.dma_start(out_words[:, EARLY], res_codes[:, EARLY])
        quantise(LATE)
        nc.sync.dma_start(out_words[:, LATE], res_codes[:, LATE])
        for q in range(4):
            (nc.sync, nc.scalar)[q % 2].dma_start(out_2[0, 4 * q : 4 * q + 4, :].bitcast(I32),
                                                  res_plane[32 * q : 32 * q + 4, :].bitcast(I32))
